import numpy as np
import ml_dtypes


def mxq(x, axis, fmt="e4m3"):
    dtype, down = {"e4m3": (ml_dtypes.float8_e4m3fn, 7), "e5m2": (ml_dtypes.float8_e5m2, 14)}[fmt]
    v = np.moveaxis(np.asarray(x, np.float32).astype(ml_dtypes.bfloat16).astype(np.float64), axis, -1)
    blocks = v.reshape(v.shape[:-1] + (-1, 32))
    amax = np.abs(blocks).max(-1, keepdims=True)
    byte = np.maximum(np.where(amax > 0, np.frexp(amax)[1] - 1 + 127, 0) - down, 1)
    scale = np.exp2(byte - 127.0)
    codes = (blocks / scale).astype(np.float32).astype(dtype).astype(np.float64)
    return np.moveaxis((codes * scale).reshape(v.shape), -1, axis)


WIDE = False


def mx_kscale(k):
    if not WIDE:
        return np.ones(k)
    levels = np.array([10, -10, 5, -5, 0])
    if k % 512:
        return np.exp2(np.random.permutation(np.resize(levels, k // 32))).repeat(32)
    a = np.empty((k // 512, 16))
    for p in range(k // 512):
        a[p, :8] = np.random.permutation(np.resize(levels, 8))
        for g in range(8):
            far = levels[np.abs(levels - a[p, g]) >= 10]
            a[p, g + 8] = far[np.random.randint(len(far))]
    return np.exp2(a.ravel()).repeat(32)


def f64(x):
    return np.asarray(x).astype(np.float64)


def striped8(idx):
    return np.asarray(idx).reshape(8, -1, 16).transpose(0, 2, 1).reshape(128, -1).astype(np.uint16)


def unstriped8(offs):
    return offs.reshape(8, 16, -1).transpose(0, 2, 1).reshape(8, -1).astype(np.int64)


def pick8(x, idx, run):
    r = np.arange(len(x))
    return x[r[:, None], idx[r % (8 * run) // run]]


E2M1 = np.array([0.0, 0.5, 1.0, 1.5, 2.0, 3.0, 4.0, 6.0, -0.0, -0.5, -1.0, -1.5, -2.0, -3.0, -4.0, -6.0])


def pack_weight(w, fmt):
    k, n = w.shape
    w = f64(np.asarray(w, np.float32).astype(ml_dtypes.bfloat16)).reshape(k // 32, 32, n)
    amax = np.abs(w).max(1)
    if fmt == "e4m3":
        byte = np.frexp(amax)[1] - 1 + 127 - 7
    else:
        mant, ex = np.frexp(amax / 6.0)
        byte = np.where(mant > 0.5, ex, ex - 1) + 127
    byte = np.clip(np.where(amax > 0, byte, 1), 1, 254)
    scaled = (w * np.exp2(127.0 - byte)[:, None, :]).reshape(k, n).astype(np.float32)
    by_word = np.ascontiguousarray(scaled.reshape(k // 512, 128, 4, n).transpose(0, 1, 3, 2))
    if fmt == "e4m3":
        words = by_word.astype(ml_dtypes.float8_e4m3fn).view(np.uint8)
    else:
        c = by_word.astype(ml_dtypes.float4_e2m1fn).view(np.uint8) & 0xF
        words = (c[..., 0::2] | (c[..., 1::2] << 4)).reshape(k // 512, 128, 2 * n)
    return np.ascontiguousarray(words), np.ascontiguousarray(byte.astype(np.uint8).reshape(k // 512, 16, n))


def unpack_weight(words, scales, fmt):
    g, _, n = scales.shape
    words = np.ascontiguousarray(words).reshape(g, 128, n, -1)
    if fmt == "e4m3":
        vals = words.view(ml_dtypes.float8_e4m3fn).astype(np.float64)
    else:
        nib = np.empty((g, 128, n, 4), np.uint8)
        nib[..., 0::2] = words & 0xF
        nib[..., 1::2] = words >> 4
        vals = E2M1[nib]
    vals = vals * np.repeat(np.exp2(scales.astype(np.float64) - 127.0), 8, axis=1)[..., None]
    return vals.transpose(0, 1, 3, 2).reshape(g * 512, n)


def sigmoid(v):
    return 1.0 / (1.0 + np.exp(-v))


D, V, Q, I = 512, 2048, 128, 512


def setup_inputs():
    n = np.random.standard_normal
    idx = np.stack([np.random.permutation(V)[:I] for _ in range(8)])
    idx2 = np.stack([np.random.permutation(V)[:I] for _ in range(8)])
    fd = mx_kscale(D)
    vocp = pack_weight(n((D, V)) / fd[:, None], "e2m1")
    return {
        "hid": (n((D, Q)) * 1.0 / np.sqrt(D) * fd[:, None]).astype(np.float32),
        "voc_words": vocp[0],
        "voc_scales": vocp[1],
        "sw": (np.random.uniform(0.5, 2.0, (1, I))).astype(np.float32),
        "sw2": (np.random.uniform(0.5, 2.0, (1, I))).astype(np.float32),
        "saved": (np.random.uniform(-0.5, 0.5, (Q, 1))).astype(np.float32),
        "beta": (np.random.uniform(1.0, 3.0, (Q, 1))).astype(np.float32),
        "old": (0.5 * n((Q, V))).astype(np.float32),
        "offs": striped8(idx),
        "offs2": striped8(idx2),
    }


def reference(hid, voc_words, voc_scales, sw, sw2, saved, beta, old, offs, offs2):
    idx = unstriped8(offs)
    idx2 = unstriped8(offs2)
    vocu = unpack_weight(voc_words, voc_scales, "e2m1")
    hidq = mxq(f64(hid), 0, "e4m3")
    a = hidq.T @ vocu
    m1 = np.max(a, axis=1, keepdims=True)
    px = np.exp(pick8(a, idx, 16) - m1)
    px2 = np.exp(pick8(a, idx2, 16) - m1)
    s1l = np.sum(px * f64(sw), axis=1, keepdims=True)
    s2l = np.sum(px2 * f64(sw2), axis=1, keepdims=True)
    dl = np.log(s1l) - np.log(s2l) - f64(saved)
    ddl = sigmoid(dl * f64(beta) * (-1.0)) * f64(beta)
    ds2l = ddl * (-1.0) / s2l
    ds1l = ddl / s1l
    dpx2 = ds2l * f64(sw2)
    dpx = ds1l * f64(sw)
    e1 = dpx2 * px2
    s1 = np.zeros((Q, V))
    s1[np.arange(Q)[:, None], idx2[np.arange(Q) % 128 // 16]] = e1
    e2 = dpx * px
    s2 = np.zeros((Q, V))
    s2[np.arange(Q)[:, None], idx[np.arange(Q) % 128 // 16]] = e2
    da = s1 + s2
    y = da * 256.0 + f64(old)
    return y

@@ -1,0 +1,184 @@
+from contextlib import ExitStack
+
+import concourse.mybir as mybir
+from concourse.masks import make_identity
+
+F32 = mybir.dt.float32
+BF16 = mybir.dt.bfloat16
+I32 = mybir.dt.int32
+U32 = mybir.dt.uint32
+U16 = mybir.dt.uint16
+U8 = mybir.dt.uint8
+FP8X4 = mybir.dt.float8_e4m3fn_x4
+FP4X4 = mybir.dt.float4_e2m1fn_x4
+ALU = mybir.AluOpType
+ACT = mybir.ActivationFunctionType
+AXIS = mybir.AxisListType
+
+P = 128
+D, V, Q, I = 512, 2048, 128, 512
+PACK = 4
+BANK = 512
+CHUNKS = V // BANK
+BLOCKS = BANK // P
+NPE = 4
+FLOPS = 2 * D * V * Q
+
+
+def tile_attend_bodds_heads_kernel(tc, hid, voc_words, voc_scales, sw, sw2, saved, beta, old, offs, offs2, out):
+    nc = tc.nc
+    with ExitStack() as ctx:
+        sb = ctx.enter_context(tc.tile_pool(name="sb", bufs=1))
+        ps = ctx.enter_context(tc.psum_pool(name="ps", bufs=1))
+
+        list1 = sb.tile([P, I // 16], U16, name="list1")
+        list2 = sb.tile([P, I // 16], U16, name="list2")
+        hid_raw = sb.tile([P, PACK, Q], F32, name="hid_raw")
+        words = [sb.tile([P, 4 * BANK], U8, name="words%d" % h, align_bytes=64) for h in range(2)]
+        voc_plane = sb.tile([P, V], U8, name="voc_plane", align_bytes=64)
+        sw_cols = [sb.tile([P, PACK], F32, name="sw_cols%d" % n) for n in range(2)]
+        beta_sb = sb.tile([P, 1], F32, name="beta_sb")
+        saved_sb = sb.tile([P, 1], F32, name="saved_sb")
+        old_sb = [sb.tile([P, 2 * BANK], F32, name="old%d" % h) for h in range(2)]
+        placed1 = sb.tile([P, V], F32, name="placed1")
+
+        nc.vector.memset(voc_plane[:].bitcast(I32), 0)
+        nc.sync.dma_start(out=hid_raw[:], in_=hid.rearrange("(p t) q -> p t q", t=PACK))
+        for h in range(2):
+            nc.sync.dma_start(out=words[h][:].bitcast(I32), in_=voc_words[0][:, 4 * BANK * h : 4 * BANK * (h + 1)].bitcast(I32))
+        for quad in range(4):
+            nc.sync.dma_start(
+                out=voc_plane[32 * quad : 32 * quad + 4, :].bitcast(I32),
+                in_=voc_scales[0][4 * quad : 4 * quad + 4, :].bitcast(I32),
+            )
+        nc.sync.dma_start(list1[:], offs)
+        nc.sync.dma_start(list2[:], offs2)
+        nc.sync.dma_start(out=beta_sb[:], in_=beta)
+        nc.sync.dma_start(out=saved_sb[:], in_=saved)
+        for cols, src in zip(sw_cols, (sw, sw2)):
+            nc.sync.dma_start(out=cols[:], in_=src.rearrange("o (p t) -> (o p) t", t=PACK))
+        for h in range(2):
+            nc.sync.dma_start(out=old_sb[h][:], in_=old[:, 2 * BANK * h : 2 * BANK * (h + 1)])
+
+        nc.vector.memset(placed1[:], 0.0)
+        ident = sb.tile([P, P], F32, name="ident")
+        make_identity(nc, ident[:])
+
+        hid_bf = sb.tile([P, Q, PACK], BF16, name="hid_bf", tag="early", align_bytes=64)
+        hid_codes = sb.tile([P, Q], U32, name="hid_codes", align_bytes=64)
+        hid_plane = sb.tile([P, Q], U8, name="hid_plane", align_bytes=64)
+        nc.vector.tensor_copy(out=hid_bf[:], in_=hid_raw[:].rearrange("p t q -> p q t"))
+        nc.vector.quantize_mx(out=hid_codes[:].bitcast(FP8X4), scales=hid_plane[:], in_=hid_bf[:].rearrange("p q t -> p (q t)"))
+
+        placed2 = sb.tile([P, V], F32, name="placed2", tag="early", align_bytes=64)
+        nc.gpsimd.memset(placed2[:], 0.0)
+
+        beta_saved = sb.tile([P, 1], F32, name="beta_saved")
+        gain = sb.tile([P, 2], F32, name="gain")
+        nc.scalar.activation(out=beta_saved[:], in_=saved_sb[:], func=ACT.Copy, scale=beta_sb[:])
+        nc.scalar.activation(out=gain[:, 0:1], in_=beta_sb[:], func=ACT.Copy, scale=256.0)
+        nc.scalar.activation(out=gain[:, 1:2], in_=beta_sb[:], func=ACT.Copy, scale=-256.0)
+
+        scores = sb.tile([P, V], F32, name="scores")
+        chunk_max = sb.tile([P, CHUNKS], F32, name="chunk_max")
+        for c in range(CHUNKS):
+            acc = ps.tile([P, BANK], F32, name="acc%d" % c, tag="bank%d" % c)
+            w = words[c // 2][:, 2 * BANK * (c % 2) : 2 * BANK * (c % 2 + 1)]
+            nc.tensor.matmul_mx(
+                out=acc[:],
+                lhsT=hid_codes[:].bitcast(FP8X4),
+                lhsT_scale=hid_plane[:],
+                rhs=w.bitcast(FP4X4),
+                rhs_scale=voc_plane[:, BANK * c : BANK * (c + 1)],
+                start=True,
+                stop=True,
+            )
+            nc.vector.tensor_scalar(
+                out=scores[:, BANK * c : BANK * (c + 1)], in0=acc[:], scalar1=1.0, scalar2=None,
+                op0=ALU.mult, op1=ALU.max, accum_out=chunk_max[:, c : c + 1],
+            )
+        neg_max = sb.tile([P, 1], F32, name="neg_max")
+        nc.vector.tensor_reduce(out=neg_max[:], in_=chunk_max[:], axis=AXIS.X, op=ALU.max, negate=True)
+
+        sw_rows = []
+        for n in range(2):
+            rows = ps.tile([P, PACK, P], F32, name="sw_rows%d" % n)
+            for t in range(PACK):
+                nc.tensor.transpose(rows[:, t, :], sw_cols[n][:, t : t + 1].to_broadcast([P, P]), ident[:])
+            sw_rows.append(rows)
+
+        px1 = sb.tile([P, I], F32, name="px1")
+        px2 = sb.tile([P, I], F32, name="px2")
+        picked2 = sb.tile([P, I], F32, name="picked2")
+        picked1 = sb.tile([P, I], F32, name="picked1")
+        nc.vector.tensor_copy(out=picked1[:], in_=scores[:].indirect(list1[:]))
+        nc.vector.tensor_copy(out=picked2[:], in_=scores[:].indirect(list2[:]))
+        nc.scalar.activation(out=px1[:], in_=picked1[:], func=ACT.Exp, bias=neg_max[:])
+        nc.scalar.activation(out=px2[:], in_=picked2[:], func=ACT.Exp, bias=neg_max[:])
+
+        stats = sb.tile([P, 4], F32, name="stats")
+        weighted = []
+        for n, px in enumerate((px1, px2)):
+            pw = sb.tile([P, I], F32, name="weighted%d" % n)
+            nc.vector.scalar_tensor_tensor(
+                out=pw[:].rearrange("q (p t) -> q p t", t=PACK),
+                in0=px[:].rearrange("q (p t) -> q p t", t=PACK),
+                scalar=placed1[:, 0:1],
+                in1=sw_rows[n][:].rearrange("q t p -> q p t"),
+                op0=ALU.add, op1=ALU.mult, accum_out=stats[:, n : n + 1],
+            )
+            weighted.append(pw)
+        nc.vector.reciprocal(out=stats[:, 2:4], in_=stats[:, 0:2])
+        nc.vector.tensor_copy(out=placed1[:].indirect(list1[:]), in_=weighted[0][:])
+        nc.vector.tensor_copy(out=placed2[:].indirect(list2[:]), in_=weighted[1][:])
+
+        logs = sb.tile([P, 2], F32, name="logs")
+        neg_odds = sb.tile([P, 1], F32, name="neg_odds")
+        quot = sb.tile([P, 2], F32, name="quot")
+        sig = sb.tile([P, 1], F32, name="sig")
+        coef = sb.tile([P, 2], F32, name="coef")
+        nc.scalar.activation(out=logs[:], in_=stats[:, 1:3], func=ACT.Ln, accum_out=neg_odds[:])
+        for n in range(2):
+            nc.scalar.activation(out=quot[:, n : n + 1], in_=stats[:, 2 + n : 3 + n], func=ACT.Copy, scale=gain[:, n : n + 1])
+        nc.scalar.activation(out=sig[:], in_=neg_odds[:], func=ACT.Sigmoid, scale=beta_sb[:], bias=beta_saved[:])
+        nc.scalar.activation(out=coef[:], in_=quot[:], func=ACT.Copy, scale=sig[:])
+
+        def old_cols(c, a, b):
+            return old_sb[c // 2][:, BANK * (c % 2) + a : BANK * (c % 2) + b]
+
+        turned = []
+        for c in range(NPE):
+            bank = ps.tile([P, BLOCKS, P], F32, name="turned%d" % c, tag="bank%d" % c)
+            for b in range(BLOCKS):
+                nc.tensor.matmul(bank[:, b, :], lhsT=old_cols(c, P * b, P * (b + 1)), rhs=ident[:], is_transpose=True, start=(b == 0), stop=False)
+            turned.append(bank)
+        partial = []
+
+        def scale_and_turn(c):
+            scaled = sb.tile([P, BANK], F32, name="scaled%d" % c)
+            nc.scalar.activation(out=scaled[:], in_=placed1[:, BANK * c : BANK * (c + 1)], func=ACT.Copy, scale=coef[:, 0:1])
+            for b in range(BLOCKS):
+                nc.tensor.matmul(turned[c][:, b, :], lhsT=scaled[:, P * b : P * (b + 1)], rhs=ident[:], is_transpose=True, start=False, stop=(b == BLOCKS - 1))
+
+        def turn_back(c):
+            back = sb.tile([P, BLOCKS, P], F32, name="back%d" % c)
+            nc.scalar.copy(out=back[:], in_=turned[c][:])
+            part = ps.tile([P, BLOCKS, P], F32, name="part%d" % c, tag="bank%d" % c)
+            for b in range(BLOCKS):
+                nc.tensor.transpose(part[:, b, :], back[:, b, :], ident[:])
+            partial.append(part[:].rearrange("q b p -> q (b p)"))
+
+        for c in range(NPE + 1):
+            if c < NPE:
+                scale_and_turn(c)
+            if c > 0:
+                turn_back(c - 1)
+        for c in range(CHUNKS):
+            cols = slice(BANK * c, BANK * (c + 1))
+            if c >= NPE:
+                part = sb.tile([P, BANK], F32, name="vpart%d" % c)
+                nc.vector.scalar_tensor_tensor(out=part[:], in0=placed1[:, cols], scalar=coef[:, 0:1], in1=old_cols(c, 0, BANK), op0=ALU.mult, op1=ALU.add)
+                partial.append(part[:])
+            res = sb.tile([P, BANK], F32, name="res%d" % c)
+            nc.vector.scalar_tensor_tensor(out=res[:], in0=placed2[:, cols], scalar=coef[:, 1:2], in1=partial[c], op0=ALU.mult, op1=ALU.add)
+            nc.sync.dma_start(out=out[:, cols], in_=res[:])

@@ -21,7 +21,9 @@ PACK = 4
 BANK = 512
 CHUNKS = V // BANK
 BLOCKS = BANK // P
-NPE = 4
+NPE = 3
+WORD_LOADS = (1, 1, 2)
+PIECES = ((0, 0, 512), (3, 0, 512), (1, 0, 512), (2, 0, 256), (2, 256, 512))
 FLOPS = 2 * D * V * Q
 
 
@@ -34,7 +36,7 @@ def tile_attend_bodds_heads_kernel(tc, hid, voc_words, voc_scales, sw, sw2, save
         list1 = sb.tile([P, I // 16], U16, name="list1")
         list2 = sb.tile([P, I // 16], U16, name="list2")
         hid_raw = sb.tile([P, PACK, Q], F32, name="hid_raw")
-        words = [sb.tile([P, 4 * BANK], U8, name="words%d" % h, align_bytes=64) for h in range(2)]
+        words = [sb.tile([P, 2 * BANK * n], U8, name="words%d" % h, align_bytes=64) for h, n in enumerate(WORD_LOADS)]
         voc_plane = sb.tile([P, V], U8, name="voc_plane", align_bytes=64)
         sw_cols = [sb.tile([P, PACK], F32, name="sw_cols%d" % n) for n in range(2)]
         beta_sb = sb.tile([P, 1], F32, name="beta_sb")
@@ -42,15 +44,19 @@ def tile_attend_bodds_heads_kernel(tc, hid, voc_words, voc_scales, sw, sw2, save
         old_sb = [sb.tile([P, 2 * BANK], F32, name="old%d" % h) for h in range(2)]
         placed1 = sb.tile([P, V], F32, name="placed1")
 
-        nc.vector.memset(voc_plane[:].bitcast(I32), 0)
+        nc.gpsimd.memset(voc_plane[:].bitcast(I32), 0)
         nc.sync.dma_start(out=hid_raw[:], in_=hid.rearrange("(p t) q -> p t q", t=PACK))
-        for h in range(2):
-            nc.sync.dma_start(out=words[h][:].bitcast(I32), in_=voc_words[0][:, 4 * BANK * h : 4 * BANK * (h + 1)].bitcast(I32))
         for quad in range(4):
             nc.sync.dma_start(
                 out=voc_plane[32 * quad : 32 * quad + 4, :].bitcast(I32),
                 in_=voc_scales[0][4 * quad : 4 * quad + 4, :].bitcast(I32),
             )
+        first = 0
+        word_cols = []
+        for tile, n in zip(words, WORD_LOADS):
+            nc.sync.dma_start(out=tile[:].bitcast(I32), in_=voc_words[0][:, 2 * BANK * first : 2 * BANK * (first + n)].bitcast(I32))
+            word_cols.extend(tile[:, 2 * BANK * j : 2 * BANK * (j + 1)] for j in range(n))
+            first += n
         nc.sync.dma_start(list1[:], offs)
         nc.sync.dma_start(list2[:], offs2)
         nc.sync.dma_start(out=beta_sb[:], in_=beta)
@@ -83,7 +89,7 @@ def tile_attend_bodds_heads_kernel(tc, hid, voc_words, voc_scales, sw, sw2, save
         chunk_max = sb.tile([P, CHUNKS], F32, name="chunk_max")
         for c in range(CHUNKS):
             acc = ps.tile([P, BANK], F32, name="acc%d" % c, tag="bank%d" % c)
-            w = words[c // 2][:, 2 * BANK * (c % 2) : 2 * BANK * (c % 2 + 1)]
+            w = word_cols[c]
             nc.tensor.matmul_mx(
                 out=acc[:],
                 lhsT=hid_codes[:].bitcast(FP8X4),
@@ -128,8 +134,10 @@ def tile_attend_bodds_heads_kernel(tc, hid, voc_words, voc_scales, sw, sw2, save
                 op0=ALU.add, op1=ALU.mult, accum_out=stats[:, n : n + 1],
             )
             weighted.append(pw)
-        nc.vector.reciprocal(out=stats[:, 2:4], in_=stats[:, 0:2])
+            if n == 0:
+                nc.vector.reciprocal(out=stats[:, 2:3], in_=stats[:, 0:1])
         nc.vector.tensor_copy(out=placed1[:].indirect(list1[:]), in_=weighted[0][:])
+        nc.vector.reciprocal(out=stats[:, 3:4], in_=stats[:, 1:2])
         nc.vector.tensor_copy(out=placed2[:].indirect(list2[:]), in_=weighted[1][:])
 
         logs = sb.tile([P, 2], F32, name="logs")
@@ -138,10 +146,11 @@ def tile_attend_bodds_heads_kernel(tc, hid, voc_words, voc_scales, sw, sw2, save
         sig = sb.tile([P, 1], F32, name="sig")
         coef = sb.tile([P, 2], F32, name="coef")
         nc.scalar.activation(out=logs[:], in_=stats[:, 1:3], func=ACT.Ln, accum_out=neg_odds[:])
-        for n in range(2):
-            nc.scalar.activation(out=quot[:, n : n + 1], in_=stats[:, 2 + n : 3 + n], func=ACT.Copy, scale=gain[:, n : n + 1])
+        nc.scalar.activation(out=quot[:, 0:1], in_=stats[:, 2:3], func=ACT.Copy, scale=gain[:, 0:1])
         nc.scalar.activation(out=sig[:], in_=neg_odds[:], func=ACT.Sigmoid, scale=beta_sb[:], bias=beta_saved[:])
-        nc.scalar.activation(out=coef[:], in_=quot[:], func=ACT.Copy, scale=sig[:])
+        nc.scalar.activation(out=coef[:, 0:1], in_=quot[:, 0:1], func=ACT.Copy, scale=sig[:])
+        nc.scalar.activation(out=quot[:, 1:2], in_=gain[:, 1:2], func=ACT.Copy, scale=sig[:])
+        nc.scalar.activation(out=coef[:, 1:2], in_=stats[:, 3:4], func=ACT.Copy, scale=quot[:, 1:2])
 
         def old_cols(c, a, b):
             return old_sb[c // 2][:, BANK * (c % 2) + a : BANK * (c % 2) + b]
@@ -161,24 +170,22 @@ def tile_attend_bodds_heads_kernel(tc, hid, voc_words, voc_scales, sw, sw2, save
                 nc.tensor.matmul(turned[c][:, b, :], lhsT=scaled[:, P * b : P * (b + 1)], rhs=ident[:], is_transpose=True, start=False, stop=(b == BLOCKS - 1))
 
         def turn_back(c):
-            back = sb.tile([P, BLOCKS, P], F32, name="back%d" % c)
+            back = sb.tile([P, BLOCKS, P], F32, name="back%d" % c, tag="back%d" % c)
             nc.scalar.copy(out=back[:], in_=turned[c][:])
             part = ps.tile([P, BLOCKS, P], F32, name="part%d" % c, tag="bank%d" % c)
             for b in range(BLOCKS):
                 nc.tensor.transpose(part[:, b, :], back[:, b, :], ident[:])
             partial.append(part[:].rearrange("q b p -> q (b p)"))
 
-        for c in range(NPE + 1):
-            if c < NPE:
-                scale_and_turn(c)
-            if c > 0:
-                turn_back(c - 1)
-        for c in range(CHUNKS):
-            cols = slice(BANK * c, BANK * (c + 1))
-            if c >= NPE:
-                part = sb.tile([P, BANK], F32, name="vpart%d" % c)
-                nc.vector.scalar_tensor_tensor(out=part[:], in0=placed1[:, cols], scalar=coef[:, 0:1], in1=old_cols(c, 0, BANK), op0=ALU.mult, op1=ALU.add)
+        for c in range(NPE):
+            scale_and_turn(c)
+        for c in range(NPE):
+            turn_back(c)
+        for c, a, b in PIECES:
+            if c == len(partial):
+                part = sb.tile([P, BANK], F32, name="vpart%d" % c, tag="back%d" % (c - NPE))
+                nc.vector.scalar_tensor_tensor(out=part[:], in0=placed1[:, BANK * c : BANK * (c + 1)], scalar=coef[:, 0:1], in1=old_cols(c, 0, BANK), op0=ALU.mult, op1=ALU.add)
                 partial.append(part[:])
-            res = sb.tile([P, BANK], F32, name="res%d" % c)
-            nc.vector.scalar_tensor_tensor(out=res[:], in0=placed2[:, cols], scalar=coef[:, 1:2], in1=partial[c], op0=ALU.mult, op1=ALU.add)
-            nc.sync.dma_start(out=out[:, cols], in_=res[:])
+            res = sb.tile([P, b - a], F32, name="res%d_%d" % (c, a))
+            nc.vector.scalar_tensor_tensor(out=res[:], in0=placed2[:, BANK * c + a : BANK * c + b], scalar=coef[:, 1:2], in1=partial[c][:, a:b], op0=ALU.mult, op1=ALU.add)
+            nc.sync.dma_start(out=out[:, BANK * c + a : BANK * c + b], in_=res[:])

@@ -19,11 +19,12 @@ P = 128
 D, V, Q, I = 512, 2048, 128, 512
 PACK = 4
 BANK = 512
-CHUNKS = V // BANK
-BLOCKS = BANK // P
-NPE = 3
-WORD_LOADS = (1, 1, 2)
-PIECES = ((0, 0, 512), (3, 0, 512), (1, 0, 512), (2, 0, 256), (2, 256, 512))
+WORD_LOADS = (512, 512, 1024)
+PASSES = (512, 512, 512, 512)
+TURNED = ((0, 512), (512, 512), (1024, 512))
+ACT_ORDER = (("u", 0), ("u", 1), ("u", 2), ("c", 0), ("c", 1), ("c", 2))
+DIRECT = ((1536, 128), (1664, 384))
+FINAL = ((0, 512), (512, 512), (1024, 384), (1408, 128))
 FLOPS = 2 * D * V * Q
 
 
@@ -35,8 +36,8 @@ def tile_attend_bodds_heads_kernel(tc, hid, voc_words, voc_scales, sw, sw2, save
 
         list1 = sb.tile([P, I // 16], U16, name="list1")
         list2 = sb.tile([P, I // 16], U16, name="list2")
-        hid_raw = sb.tile([P, PACK, Q], F32, name="hid_raw")
-        words = [sb.tile([P, 2 * BANK * n], U8, name="words%d" % h, align_bytes=64) for h, n in enumerate(WORD_LOADS)]
+        hid_raw = sb.tile([P, PACK, Q], F32, name="hid_raw", tag="raw")
+        words = [sb.tile([P, 2 * n], U8, name="words%d" % h, tag="words%d" % h, align_bytes=64) for h, n in enumerate(WORD_LOADS)]
         voc_plane = sb.tile([P, V], U8, name="voc_plane", align_bytes=64)
         sw_cols = [sb.tile([P, PACK], F32, name="sw_cols%d" % n) for n in range(2)]
         beta_sb = sb.tile([P, 1], F32, name="beta_sb")
@@ -44,7 +45,7 @@ def tile_attend_bodds_heads_kernel(tc, hid, voc_words, voc_scales, sw, sw2, save
         old_sb = [sb.tile([P, 2 * BANK], F32, name="old%d" % h) for h in range(2)]
         placed1 = sb.tile([P, V], F32, name="placed1")
 
-        nc.gpsimd.memset(voc_plane[:].bitcast(I32), 0)
+        nc.vector.memset(voc_plane[:].bitcast(I32), 0)
         nc.sync.dma_start(out=hid_raw[:], in_=hid.rearrange("(p t) q -> p t q", t=PACK))
         for quad in range(4):
             nc.sync.dma_start(
@@ -52,11 +53,17 @@ def tile_attend_bodds_heads_kernel(tc, hid, voc_words, voc_scales, sw, sw2, save
                 in_=voc_scales[0][4 * quad : 4 * quad + 4, :].bitcast(I32),
             )
         first = 0
-        word_cols = []
         for tile, n in zip(words, WORD_LOADS):
-            nc.sync.dma_start(out=tile[:].bitcast(I32), in_=voc_words[0][:, 2 * BANK * first : 2 * BANK * (first + n)].bitcast(I32))
-            word_cols.extend(tile[:, 2 * BANK * j : 2 * BANK * (j + 1)] for j in range(n))
+            nc.sync.dma_start(out=tile[:].bitcast(I32), in_=voc_words[0][:, 2 * first : 2 * (first + n)].bitcast(I32))
             first += n
+
+        def word_cols(a, b):
+            first = 0
+            for tile, n in zip(words, WORD_LOADS):
+                if a < first + n:
+                    return tile[:, 2 * (a - first) : 2 * (b - first)]
+                first += n
+
         nc.sync.dma_start(list1[:], offs)
         nc.sync.dma_start(list2[:], offs2)
         nc.sync.dma_start(out=beta_sb[:], in_=beta)
@@ -66,9 +73,7 @@ def tile_attend_bodds_heads_kernel(tc, hid, voc_words, voc_scales, sw, sw2, save
         for h in range(2):
             nc.sync.dma_start(out=old_sb[h][:], in_=old[:, 2 * BANK * h : 2 * BANK * (h + 1)])
 
-        nc.vector.memset(placed1[:], 0.0)
-        ident = sb.tile([P, P], F32, name="ident")
-        make_identity(nc, ident[:])
+        nc.vector.memset(placed1[:, : 2048], 0.0)
 
         hid_bf = sb.tile([P, Q, PACK], BF16, name="hid_bf", tag="early", align_bytes=64)
         hid_codes = sb.tile([P, Q], U32, name="hid_codes", align_bytes=64)
@@ -76,6 +81,8 @@ def tile_attend_bodds_heads_kernel(tc, hid, voc_words, voc_scales, sw, sw2, save
         nc.vector.tensor_copy(out=hid_bf[:], in_=hid_raw[:].rearrange("p t q -> p q t"))
         nc.vector.quantize_mx(out=hid_codes[:].bitcast(FP8X4), scales=hid_plane[:], in_=hid_bf[:].rearrange("p q t -> p (q t)"))
 
+        ident = sb.tile([P, P], F32, name="ident", tag="words0", align_bytes=64)
+        make_identity(nc, ident[:])
         placed2 = sb.tile([P, V], F32, name="placed2", tag="early", align_bytes=64)
         nc.gpsimd.memset(placed2[:], 0.0)
 
@@ -86,23 +93,24 @@ def tile_attend_bodds_heads_kernel(tc, hid, voc_words, voc_scales, sw, sw2, save
         nc.scalar.activation(out=gain[:, 1:2], in_=beta_sb[:], func=ACT.Copy, scale=-256.0)
 
         scores = sb.tile([P, V], F32, name="scores")
-        chunk_max = sb.tile([P, CHUNKS], F32, name="chunk_max")
-        for c in range(CHUNKS):
-            acc = ps.tile([P, BANK], F32, name="acc%d" % c, tag="bank%d" % c)
-            w = word_cols[c]
+        chunk_max = sb.tile([P, len(PASSES)], F32, name="chunk_max")
+        first = 0
+        for c, n in enumerate(PASSES):
+            acc = ps.tile([P, n], F32, name="acc%d" % c, tag="bank%d" % c)
             nc.tensor.matmul_mx(
                 out=acc[:],
                 lhsT=hid_codes[:].bitcast(FP8X4),
                 lhsT_scale=hid_plane[:],
-                rhs=w.bitcast(FP4X4),
-                rhs_scale=voc_plane[:, BANK * c : BANK * (c + 1)],
+                rhs=word_cols(first, first + n).bitcast(FP4X4),
+                rhs_scale=voc_plane[:, first : first + n],
                 start=True,
                 stop=True,
             )
             nc.vector.tensor_scalar(
-                out=scores[:, BANK * c : BANK * (c + 1)], in0=acc[:], scalar1=1.0, scalar2=None,
+                out=scores[:, first : first + n], in0=acc[:], scalar1=1.0, scalar2=None,
                 op0=ALU.mult, op1=ALU.max, accum_out=chunk_max[:, c : c + 1],
             )
+            first += n
         neg_max = sb.tile([P, 1], F32, name="neg_max")
         nc.vector.tensor_reduce(out=neg_max[:], in_=chunk_max[:], axis=AXIS.X, op=ALU.max, negate=True)
 
@@ -115,8 +123,8 @@ def tile_attend_bodds_heads_kernel(tc, hid, voc_words, voc_scales, sw, sw2, save
 
         px1 = sb.tile([P, I], F32, name="px1")
         px2 = sb.tile([P, I], F32, name="px2")
-        picked2 = sb.tile([P, I], F32, name="picked2")
         picked1 = sb.tile([P, I], F32, name="picked1")
+        picked2 = sb.tile([P, I], F32, name="picked2")
         nc.vector.tensor_copy(out=picked1[:], in_=scores[:].indirect(list1[:]))
         nc.vector.tensor_copy(out=picked2[:], in_=scores[:].indirect(list2[:]))
         nc.scalar.activation(out=px1[:], in_=picked1[:], func=ACT.Exp, bias=neg_max[:])
@@ -136,56 +144,61 @@ def tile_attend_bodds_heads_kernel(tc, hid, voc_words, voc_scales, sw, sw2, save
             weighted.append(pw)
             if n == 0:
                 nc.vector.reciprocal(out=stats[:, 2:3], in_=stats[:, 0:1])
+        quot = sb.tile([P, 2], F32, name="quot")
+        nc.vector.tensor_scalar(out=quot[:, 0:1], in0=stats[:, 2:3], scalar1=gain[:, 0:1], scalar2=None, op0=ALU.mult)
         nc.vector.tensor_copy(out=placed1[:].indirect(list1[:]), in_=weighted[0][:])
         nc.vector.reciprocal(out=stats[:, 3:4], in_=stats[:, 1:2])
         nc.vector.tensor_copy(out=placed2[:].indirect(list2[:]), in_=weighted[1][:])
 
         logs = sb.tile([P, 2], F32, name="logs")
         neg_odds = sb.tile([P, 1], F32, name="neg_odds")
-        quot = sb.tile([P, 2], F32, name="quot")
         sig = sb.tile([P, 1], F32, name="sig")
         coef = sb.tile([P, 2], F32, name="coef")
         nc.scalar.activation(out=logs[:], in_=stats[:, 1:3], func=ACT.Ln, accum_out=neg_odds[:])
-        nc.scalar.activation(out=quot[:, 0:1], in_=stats[:, 2:3], func=ACT.Copy, scale=gain[:, 0:1])
         nc.scalar.activation(out=sig[:], in_=neg_odds[:], func=ACT.Sigmoid, scale=beta_sb[:], bias=beta_saved[:])
         nc.scalar.activation(out=coef[:, 0:1], in_=quot[:, 0:1], func=ACT.Copy, scale=sig[:])
-        nc.scalar.activation(out=quot[:, 1:2], in_=gain[:, 1:2], func=ACT.Copy, scale=sig[:])
-        nc.scalar.activation(out=coef[:, 1:2], in_=stats[:, 3:4], func=ACT.Copy, scale=quot[:, 1:2])
+        coef2 = sb.tile([P, 1], F32, name="coef2")
+        nc.vector.scalar_tensor_tensor(out=coef2[:], in0=stats[:, 3:4], scalar=gain[:, 1:2], in1=sig[:], op0=ALU.mult, op1=ALU.mult)
 
-        def old_cols(c, a, b):
-            return old_sb[c // 2][:, BANK * (c % 2) + a : BANK * (c % 2) + b]
+        def old_cols(a, b):
+            h = a // (2 * BANK)
+            return old_sb[h][:, a - 2 * BANK * h : b - 2 * BANK * h]
 
         turned = []
-        for c in range(NPE):
-            bank = ps.tile([P, BLOCKS, P], F32, name="turned%d" % c, tag="bank%d" % c)
-            for b in range(BLOCKS):
-                nc.tensor.matmul(bank[:, b, :], lhsT=old_cols(c, P * b, P * (b + 1)), rhs=ident[:], is_transpose=True, start=(b == 0), stop=False)
+        for c, (a, n) in enumerate(TURNED):
+            bank = ps.tile([P, n], F32, name="turned%d" % c, tag="bank%d" % c)
+            for b in range(0, n, P):
+                nc.tensor.matmul(bank[:, b : b + P], lhsT=old_cols(a + b, a + b + P), rhs=ident[:], is_transpose=True, start=(b == 0), stop=False)
             turned.append(bank)
-        partial = []
+        partial = {}
+        keep = {}
+        for kind, c in ACT_ORDER:
+            a, n = TURNED[c]
+            if kind == "u":
+                scaled = sb.tile([P, n], F32, name="scaled%d" % c)
+                keep["u%d" % c] = scaled
+                nc.scalar.activation(out=scaled[:], in_=placed1[:, a : a + n], func=ACT.Copy, scale=coef[:, 0:1])
+                for b in range(0, n, P):
+                    nc.tensor.matmul(turned[c][:, b : b + P], lhsT=scaled[:, b : b + P], rhs=ident[:], is_transpose=True, start=False, stop=(b == n - P))
+            else:
+                back = sb.tile([P, n], F32, name="back%d" % c)
+                keep["c%d" % c] = back
+                nc.scalar.copy(out=back[:], in_=turned[c][:])
+                part = ps.tile([P, n], F32, name="part%d" % c, tag="bank%d" % c)
+                for b in range(0, n, P):
+                    nc.tensor.transpose(part[:, b : b + P], back[:, b : b + P], ident[:])
+                partial[a] = part
 
-        def scale_and_turn(c):
-            scaled = sb.tile([P, BANK], F32, name="scaled%d" % c)
-            nc.scalar.activation(out=scaled[:], in_=placed1[:, BANK * c : BANK * (c + 1)], func=ACT.Copy, scale=coef[:, 0:1])
-            for b in range(BLOCKS):
-                nc.tensor.matmul(turned[c][:, b, :], lhsT=scaled[:, P * b : P * (b + 1)], rhs=ident[:], is_transpose=True, start=False, stop=(b == BLOCKS - 1))
+        def finish(a, b, rest):
+            res = sb.tile([P, b - a], F32, name="res%d" % a)
+            keep["r%d" % a] = res
+            nc.vector.scalar_tensor_tensor(out=res[:], in0=placed2[:, a:b], scalar=coef2[:], in1=rest, op0=ALU.mult, op1=ALU.add)
+            nc.sync.dma_start(out=out[:, a:b], in_=res[:])
 
-        def turn_back(c):
-            back = sb.tile([P, BLOCKS, P], F32, name="back%d" % c, tag="back%d" % c)
-            nc.scalar.copy(out=back[:], in_=turned[c][:])
-            part = ps.tile([P, BLOCKS, P], F32, name="part%d" % c, tag="bank%d" % c)
-            for b in range(BLOCKS):
-                nc.tensor.transpose(part[:, b, :], back[:, b, :], ident[:])
-            partial.append(part[:].rearrange("q b p -> q (b p)"))
-
-        for c in range(NPE):
-            scale_and_turn(c)
-        for c in range(NPE):
-            turn_back(c)
-        for c, a, b in PIECES:
-            if c == len(partial):
-                part = sb.tile([P, BANK], F32, name="vpart%d" % c, tag="back%d" % (c - NPE))
-                nc.vector.scalar_tensor_tensor(out=part[:], in0=placed1[:, BANK * c : BANK * (c + 1)], scalar=coef[:, 0:1], in1=old_cols(c, 0, BANK), op0=ALU.mult, op1=ALU.add)
-                partial.append(part[:])
-            res = sb.tile([P, b - a], F32, name="res%d_%d" % (c, a))
-            nc.vector.scalar_tensor_tensor(out=res[:], in0=placed2[:, BANK * c + a : BANK * c + b], scalar=coef[:, 1:2], in1=partial[c][:, a:b], op0=ALU.mult, op1=ALU.add)
-            nc.sync.dma_start(out=out[:, BANK * c + a : BANK * c + b], in_=res[:])
+        for a, n in DIRECT:
+            part = sb.tile([P, n], F32, name="vpart%d" % a)
+            nc.vector.scalar_tensor_tensor(out=part[:], in0=placed1[:, a : a + n], scalar=coef[:, 0:1], in1=old_cols(a, a + n), op0=ALU.mult, op1=ALU.add)
+            finish(a, a + n, part[:])
+        for a, n in FINAL:
+            base = BANK * (a // BANK)
+            finish(a, a + n, partial[base][:, a - base : a - base + n])

@@ -21,10 +21,10 @@ PACK = 4
 BANK = 512
 WORD_LOADS = (512, 512, 1024)
 PASSES = (512, 512, 512, 512)
-TURNED = ((0, 512), (512, 512), (1024, 512))
+TURNED = ((0, 512), (512, 512), (1024, 256))
 ACT_ORDER = (("u", 0), ("u", 1), ("u", 2), ("c", 0), ("c", 1), ("c", 2))
-DIRECT = ((1536, 128), (1664, 384))
-FINAL = ((0, 512), (512, 512), (1024, 384), (1408, 128))
+DIRECT = ((1280, 128), (1408, 640))
+FINAL = ((0, 512), (512, 512), (1024, 128), (1152, 128))
 FLOPS = 2 * D * V * Q
 
 
@@ -195,10 +195,13 @@ def tile_attend_bodds_heads_kernel(tc, hid, voc_words, voc_scales, sw, sw2, save
             nc.vector.scalar_tensor_tensor(out=res[:], in0=placed2[:, a:b], scalar=coef2[:], in1=rest, op0=ALU.mult, op1=ALU.add)
             nc.sync.dma_start(out=out[:, a:b], in_=res[:])
 
+        first, width = 1280, 768
+        pool_scaled = sb.tile([P, width], F32, name="pool_scaled")
+        pool_part = sb.tile([P, width], F32, name="pool_part")
+        nc.gpsimd.tensor_scalar(out=pool_scaled[:], in0=placed1[:, first : first + width], scalar1=coef[:, 0:1], scalar2=0.0, op0=ALU.mult, op1=ALU.add)
+        nc.gpsimd.tensor_tensor(out=pool_part[:], in0=pool_scaled[:], in1=old_cols(first, first + width), op=ALU.add)
         for a, n in DIRECT:
-            part = sb.tile([P, n], F32, name="vpart%d" % a)
-            nc.vector.scalar_tensor_tensor(out=part[:], in0=placed1[:, a : a + n], scalar=coef[:, 0:1], in1=old_cols(a, a + n), op0=ALU.mult, op1=ALU.add)
-            finish(a, a + n, part[:])
+            finish(a, a + n, pool_part[:, a - first : a - first + n])
         for a, n in FINAL:
             base = BANK * (a // BANK)
             finish(a, a + n, partial[base][:, a - base : a - base + n])

from contextlib import ExitStack

import concourse.mybir as mybir
from concourse.masks import make_identity

F32 = mybir.dt.float32
BF16 = mybir.dt.bfloat16
I32 = mybir.dt.int32
U32 = mybir.dt.uint32
U16 = mybir.dt.uint16
U8 = mybir.dt.uint8
FP8X4 = mybir.dt.float8_e4m3fn_x4
FP4X4 = mybir.dt.float4_e2m1fn_x4
ALU = mybir.AluOpType
ACT = mybir.ActivationFunctionType
AXIS = mybir.AxisListType

P = 128
D, V, Q, I = 512, 2048, 128, 512
PACK = 4
BANK = 512
WORD_LOADS = (512, 512, 1024)
PASSES = (512, 512, 512, 512)
TURNED = ((0, 512), (512, 512), (1024, 256))
ACT_ORDER = (("u", 0), ("u", 1), ("u", 2), ("c", 0), ("c", 1), ("c", 2))
DIRECT = ((1280, 128), (1408, 640))
FINAL = ((0, 512), (512, 512), (1024, 128), (1152, 128))
FLOPS = 2 * D * V * Q


def tile_attend_bodds_heads_kernel(tc, hid, voc_words, voc_scales, sw, sw2, saved, beta, old, offs, offs2, out):
    nc = tc.nc
    with ExitStack() as ctx:
        sb = ctx.enter_context(tc.tile_pool(name="sb", bufs=1))
        ps = ctx.enter_context(tc.psum_pool(name="ps", bufs=1))

        list1 = sb.tile([P, I // 16], U16, name="list1")
        list2 = sb.tile([P, I // 16], U16, name="list2")
        hid_raw = sb.tile([P, PACK, Q], F32, name="hid_raw", tag="raw")
        words = [sb.tile([P, 2 * n], U8, name="words%d" % h, tag="words%d" % h, align_bytes=64) for h, n in enumerate(WORD_LOADS)]
        voc_plane = sb.tile([P, V], U8, name="voc_plane", align_bytes=64)
        sw_cols = [sb.tile([P, PACK], F32, name="sw_cols%d" % n) for n in range(2)]
        beta_sb = sb.tile([P, 1], F32, name="beta_sb")
        saved_sb = sb.tile([P, 1], F32, name="saved_sb")
        old_sb = [sb.tile([P, 2 * BANK], F32, name="old%d" % h) for h in range(2)]
        placed1 = sb.tile([P, V], F32, name="placed1")

        nc.vector.memset(voc_plane[:].bitcast(I32), 0)
        nc.sync.dma_start(out=hid_raw[:], in_=hid.rearrange("(p t) q -> p t q", t=PACK))
        for quad in range(4):
            nc.sync.dma_start(
                out=voc_plane[32 * quad : 32 * quad + 4, :].bitcast(I32),
                in_=voc_scales[0][4 * quad : 4 * quad + 4, :].bitcast(I32),
            )
        first = 0
        for tile, n in zip(words, WORD_LOADS):
            nc.sync.dma_start(out=tile[:].bitcast(I32), in_=voc_words[0][:, 2 * first : 2 * (first + n)].bitcast(I32))
            first += n

        def word_cols(a, b):
            first = 0
            for tile, n in zip(words, WORD_LOADS):
                if a < first + n:
                    return tile[:, 2 * (a - first) : 2 * (b - first)]
                first += n

        nc.sync.dma_start(list1[:], offs)
        nc.sync.dma_start(list2[:], offs2)
        nc.sync.dma_start(out=beta_sb[:], in_=beta)
        nc.sync.dma_start(out=saved_sb[:], in_=saved)
        for cols, src in zip(sw_cols, (sw, sw2)):
            nc.sync.dma_start(out=cols[:], in_=src.rearrange("o (p t) -> (o p) t", t=PACK))
        for h in range(2):
            nc.sync.dma_start(out=old_sb[h][:], in_=old[:, 2 * BANK * h : 2 * BANK * (h + 1)])

        nc.vector.memset(placed1[:, : 2048], 0.0)

        hid_bf = sb.tile([P, Q, PACK], BF16, name="hid_bf", tag="early", align_bytes=64)
        hid_codes = sb.tile([P, Q], U32, name="hid_codes", align_bytes=64)
        hid_plane = sb.tile([P, Q], U8, name="hid_plane", align_bytes=64)
        nc.vector.tensor_copy(out=hid_bf[:], in_=hid_raw[:].rearrange("p t q -> p q t"))
        nc.vector.quantize_mx(out=hid_codes[:].bitcast(FP8X4), scales=hid_plane[:], in_=hid_bf[:].rearrange("p q t -> p (q t)"))

        ident = sb.tile([P, P], F32, name="ident", tag="words0", align_bytes=64)
        make_identity(nc, ident[:])
        placed2 = sb.tile([P, V], F32, name="placed2", tag="early", align_bytes=64)
        nc.gpsimd.memset(placed2[:], 0.0)

        beta_saved = sb.tile([P, 1], F32, name="beta_saved")
        gain = sb.tile([P, 2], F32, name="gain")
        nc.scalar.activation(out=beta_saved[:], in_=saved_sb[:], func=ACT.Copy, scale=beta_sb[:])
        nc.scalar.activation(out=gain[:, 0:1], in_=beta_sb[:], func=ACT.Copy, scale=256.0)
        nc.scalar.activation(out=gain[:, 1:2], in_=beta_sb[:], func=ACT.Copy, scale=-256.0)

        scores = sb.tile([P, V], F32, name="scores")
        chunk_max = sb.tile([P, len(PASSES)], F32, name="chunk_max")
        first = 0
        for c, n in enumerate(PASSES):
            acc = ps.tile([P, n], F32, name="acc%d" % c, tag="bank%d" % c)
            nc.tensor.matmul_mx(
                out=acc[:],
                lhsT=hid_codes[:].bitcast(FP8X4),
                lhsT_scale=hid_plane[:],
                rhs=word_cols(first, first + n).bitcast(FP4X4),
                rhs_scale=voc_plane[:, first : first + n],
                start=True,
                stop=True,
            )
            nc.vector.tensor_scalar(
                out=scores[:, first : first + n], in0=acc[:], scalar1=1.0, scalar2=None,
                op0=ALU.mult, op1=ALU.max, accum_out=chunk_max[:, c : c + 1],
            )
            first += n
        neg_max = sb.tile([P, 1], F32, name="neg_max")
        nc.vector.tensor_reduce(out=neg_max[:], in_=chunk_max[:], axis=AXIS.X, op=ALU.max, negate=True)

        sw_rows = []
        for n in range(2):
            rows = ps.tile([P, PACK, P], F32, name="sw_rows%d" % n)
            for t in range(PACK):
                nc.tensor.transpose(rows[:, t, :], sw_cols[n][:, t : t + 1].to_broadcast([P, P]), ident[:])
            sw_rows.append(rows)

        px1 = sb.tile([P, I], F32, name="px1")
        px2 = sb.tile([P, I], F32, name="px2")
        picked1 = sb.tile([P, I], F32, name="picked1")
        picked2 = sb.tile([P, I], F32, name="picked2")
        nc.vector.tensor_copy(out=picked1[:], in_=scores[:].indirect(list1[:]))
        nc.vector.tensor_copy(out=picked2[:], in_=scores[:].indirect(list2[:]))
        nc.scalar.activation(out=px1[:], in_=picked1[:], func=ACT.Exp, bias=neg_max[:])
        nc.scalar.activation(out=px2[:], in_=picked2[:], func=ACT.Exp, bias=neg_max[:])

        stats = sb.tile([P, 4], F32, name="stats")
        weighted = []
        for n, px in enumerate((px1, px2)):
            pw = sb.tile([P, I], F32, name="weighted%d" % n)
            nc.vector.scalar_tensor_tensor(
                out=pw[:].rearrange("q (p t) -> q p t", t=PACK),
                in0=px[:].rearrange("q (p t) -> q p t", t=PACK),
                scalar=placed1[:, 0:1],
                in1=sw_rows[n][:].rearrange("q t p -> q p t"),
                op0=ALU.add, op1=ALU.mult, accum_out=stats[:, n : n + 1],
            )
            weighted.append(pw)
            if n == 0:
                nc.vector.reciprocal(out=stats[:, 2:3], in_=stats[:, 0:1])
        quot = sb.tile([P, 2], F32, name="quot")
        nc.vector.tensor_scalar(out=quot[:, 0:1], in0=stats[:, 2:3], scalar1=gain[:, 0:1], scalar2=None, op0=ALU.mult)
        nc.vector.tensor_copy(out=placed1[:].indirect(list1[:]), in_=weighted[0][:])
        nc.vector.reciprocal(out=stats[:, 3:4], in_=stats[:, 1:2])
        nc.vector.tensor_copy(out=placed2[:].indirect(list2[:]), in_=weighted[1][:])

        logs = sb.tile([P, 2], F32, name="logs")
        neg_odds = sb.tile([P, 1], F32, name="neg_odds")
        sig = sb.tile([P, 1], F32, name="sig")
        coef = sb.tile([P, 2], F32, name="coef")
        nc.scalar.activation(out=logs[:], in_=stats[:, 1:3], func=ACT.Ln, accum_out=neg_odds[:])
        nc.scalar.activation(out=sig[:], in_=neg_odds[:], func=ACT.Sigmoid, scale=beta_sb[:], bias=beta_saved[:])
        nc.scalar.activation(out=coef[:, 0:1], in_=quot[:, 0:1], func=ACT.Copy, scale=sig[:])
        coef2 = sb.tile([P, 1], F32, name="coef2")
        nc.vector.scalar_tensor_tensor(out=coef2[:], in0=stats[:, 3:4], scalar=gain[:, 1:2], in1=sig[:], op0=ALU.mult, op1=ALU.mult)

        def old_cols(a, b):
            h = a // (2 * BANK)
            return old_sb[h][:, a - 2 * BANK * h : b - 2 * BANK * h]

        turned = []
        for c, (a, n) in enumerate(TURNED):
            bank = ps.tile([P, n], F32, name="turned%d" % c, tag="bank%d" % c)
            for b in range(0, n, P):
                nc.tensor.matmul(bank[:, b : b + P], lhsT=old_cols(a + b, a + b + P), rhs=ident[:], is_transpose=True, start=(b == 0), stop=False)
            turned.append(bank)
        partial = {}
        keep = {}
        for kind, c in ACT_ORDER:
            a, n = TURNED[c]
            if kind == "u":
                scaled = sb.tile([P, n], F32, name="scaled%d" % c)
                keep["u%d" % c] = scaled
                nc.scalar.activation(out=scaled[:], in_=placed1[:, a : a + n], func=ACT.Copy, scale=coef[:, 0:1])
                for b in range(0, n, P):
                    nc.tensor.matmul(turned[c][:, b : b + P], lhsT=scaled[:, b : b + P], rhs=ident[:], is_transpose=True, start=False, stop=(b == n - P))
            else:
                back = sb.tile([P, n], F32, name="back%d" % c)
                keep["c%d" % c] = back
                nc.scalar.copy(out=back[:], in_=turned[c][:])
                part = ps.tile([P, n], F32, name="part%d" % c, tag="bank%d" % c)
                for b in range(0, n, P):
                    nc.tensor.transpose(part[:, b : b + P], back[:, b : b + P], ident[:])
                partial[a] = part

        def finish(a, b, rest):
            res = sb.tile([P, b - a], F32, name="res%d" % a)
            keep["r%d" % a] = res
            nc.vector.scalar_tensor_tensor(out=res[:], in0=placed2[:, a:b], scalar=coef2[:], in1=rest, op0=ALU.mult, op1=ALU.add)
            nc.sync.dma_start(out=out[:, a:b], in_=res[:])

        first, width = 1280, 768
        pool_scaled = sb.tile([P, width], F32, name="pool_scaled")
        pool_part = sb.tile([P, width], F32, name="pool_part")
        nc.gpsimd.tensor_scalar(out=pool_scaled[:], in0=placed1[:, first : first + width], scalar1=coef[:, 0:1], scalar2=0.0, op0=ALU.mult, op1=ALU.add)
        nc.gpsimd.tensor_tensor(out=pool_part[:], in0=pool_scaled[:], in1=old_cols(first, first + width), op=ALU.add)
        for a, n in DIRECT:
            finish(a, a + n, pool_part[:, a - first : a - first + n])
        for a, n in FINAL:
            base = BANK * (a // BANK)
            finish(a, a + n, partial[base][:, a - base : a - base + n])
